import numpy as np
import ml_dtypes


def mxq(x, axis, fmt="e4m3"):
    dtype, down = {"e4m3": (ml_dtypes.float8_e4m3fn, 7), "e5m2": (ml_dtypes.float8_e5m2, 14)}[fmt]
    v = np.moveaxis(np.asarray(x, np.float32).astype(ml_dtypes.bfloat16).astype(np.float64), axis, -1)
    blocks = v.reshape(v.shape[:-1] + (-1, 32))
    amax = np.abs(blocks).max(-1, keepdims=True)
    byte = np.maximum(np.where(amax > 0, np.frexp(amax)[1] - 1 + 127, 0) - down, 1)
    scale = np.exp2(byte - 127.0)
    codes = (blocks / scale).astype(np.float32).astype(dtype).astype(np.float64)
    return np.moveaxis((codes * scale).reshape(v.shape), -1, axis)


WIDE = False


def mx_kscale(k):
    if not WIDE:
        return np.ones(k)
    levels = np.array([10, -10, 5, -5, 0])
    if k % 512:
        return np.exp2(np.random.permutation(np.resize(levels, k // 32))).repeat(32)
    a = np.empty((k // 512, 16))
    for p in range(k // 512):
        a[p, :8] = np.random.permutation(np.resize(levels, 8))
        for g in range(8):
            far = levels[np.abs(levels - a[p, g]) >= 10]
            a[p, g + 8] = far[np.random.randint(len(far))]
    return np.exp2(a.ravel()).repeat(32)


def f64(x):
    return np.asarray(x).astype(np.float64)


def striped(idx):
    return np.tile(idx.reshape(-1, 16).T, (8, 1)).astype(np.uint16)


def unstriped(offs):
    return offs[:16].T.reshape(-1).astype(np.int64)


E2M1 = np.array([0.0, 0.5, 1.0, 1.5, 2.0, 3.0, 4.0, 6.0, -0.0, -0.5, -1.0, -1.5, -2.0, -3.0, -4.0, -6.0])


def pack_weight(w, fmt):
    k, n = w.shape
    w = f64(np.asarray(w, np.float32).astype(ml_dtypes.bfloat16)).reshape(k // 32, 32, n)
    amax = np.abs(w).max(1)
    if fmt == "e4m3":
        byte = np.frexp(amax)[1] - 1 + 127 - 7
    else:
        mant, ex = np.frexp(amax / 6.0)
        byte = np.where(mant > 0.5, ex, ex - 1) + 127
    byte = np.clip(np.where(amax > 0, byte, 1), 1, 254)
    scaled = (w * np.exp2(127.0 - byte)[:, None, :]).reshape(k, n).astype(np.float32)
    by_word = np.ascontiguousarray(scaled.reshape(k // 512, 128, 4, n).transpose(0, 1, 3, 2))
    if fmt == "e4m3":
        words = by_word.astype(ml_dtypes.float8_e4m3fn).view(np.uint8)
    else:
        c = by_word.astype(ml_dtypes.float4_e2m1fn).view(np.uint8) & 0xF
        words = (c[..., 0::2] | (c[..., 1::2] << 4)).reshape(k // 512, 128, 2 * n)
    return np.ascontiguousarray(words), np.ascontiguousarray(byte.astype(np.uint8).reshape(k // 512, 16, n))


def unpack_weight(words, scales, fmt):
    g, _, n = scales.shape
    words = np.ascontiguousarray(words).reshape(g, 128, n, -1)
    if fmt == "e4m3":
        vals = words.view(ml_dtypes.float8_e4m3fn).astype(np.float64)
    else:
        nib = np.empty((g, 128, n, 4), np.uint8)
        nib[..., 0::2] = words & 0xF
        nib[..., 1::2] = words >> 4
        vals = E2M1[nib]
    vals = vals * np.repeat(np.exp2(scales.astype(np.float64) - 127.0), 8, axis=1)[..., None]
    return vals.transpose(0, 1, 3, 2).reshape(g * 512, n)


def gelu(v):
    return 0.5 * v * (1.0 + np.tanh(np.sqrt(2.0 / np.pi) * (v + 0.044715 * v**3)))


K, H, T, S, T2, P = 1536, 512, 2048, 1024, 2048, 1024

def setup_inputs():
    n = np.random.standard_normal
    s = mx_kscale(K)[:, None]
    u = mx_kscale(H)[:, None]
    d = {}
    d["tab_words"], d["tab_scales"] = pack_weight(n((K, T)) * s, "e4m3")
    d["offs"] = striped(np.random.permutation(T)[:S])
    d["w1"] = (n((K, H)) / K ** 0.5 / s * u.T).astype(np.float32)
    d["page0"] = (n((H, T2)) * u).astype(np.float32)
    d["wgs"] = np.exp(0.3 * n((128, S))).astype(np.float32)
    d["offs2"] = striped(np.random.permutation(T2)[:S])
    d["offs3"] = striped(np.random.permutation(T2)[:P])
    d["gs"] = (1.2 * np.exp(0.2 * n(H)) / u[:, 0]).astype(np.float32)
    d["lap"] = n((H, P)).astype(np.float32)
    d["gx"] = (np.exp(0.3 * n(H)) * u[:, 0]).astype(np.float32)
    d["w4_words"], d["w4_scales"] = pack_weight(1.3 * n((H, H)) / H ** 0.5 / u, "e2m1")
    d["offs4"] = striped(np.random.permutation(T2)[:P])
    d["gb"] = (0.8 * np.exp(0.3 * n(H)) / u[:, 0]).astype(np.float32)
    return d

def reference(tab_words, tab_scales, offs, w1, page0, wgs, offs2, offs3, gs, lap, gx, w4_words, w4_scales, offs4, gb):
    v = unpack_weight(tab_words, tab_scales, "e4m3")[:, unstriped(offs)]
    w4 = unpack_weight(w4_words, w4_scales, "e2m1")
    h = mxq(f64(w1), 0, "e4m3").T @ v
    page = f64(page0).copy()
    page[:, unstriped(offs2)] = np.tile(f64(wgs), (H // 128, 1)) * h
    x = np.tanh(f64(gs)[:, None] * page[:, unstriped(offs3)] + f64(lap)) * f64(gx)[:, None]
    y = w4.T @ mxq(x, 0, "e4m3")
    out = y * f64(lap) + f64(gb)[:, None] * page[:, unstriped(offs4)]
    return out

@@ -1,0 +1,295 @@
+from contextlib import ExitStack
+
+import concourse.mybir as mybir
+from concourse.masks import make_identity
+
+K, H, T, S, T2, NJ = 1536, 512, 2048, 1024, 2048, 1024
+FLOPS = 2 * K * H * S + 2 * H * H * NJ
+
+F32 = mybir.dt.float32
+BF16 = mybir.dt.bfloat16
+I32 = mybir.dt.int32
+U32 = mybir.dt.uint32
+U16 = mybir.dt.uint16
+U8 = mybir.dt.uint8
+FP8X4 = mybir.dt.float8_e4m3fn_x4
+FP4X4 = mybir.dt.float4_e2m1fn_x4
+MULT = mybir.AluOpType.mult
+ADD = mybir.AluOpType.add
+COPY = mybir.ActivationFunctionType.Copy
+TANH = mybir.ActivationFunctionType.Tanh
+
+P = 128
+PACK = 4
+PASSES = K // (P * PACK)
+BLOCKS = H // P
+HALF = 512
+HALVES = S // HALF
+LIST_COLS = HALF // 16
+RUN = 4
+W1_GROUPS = ((0, 1), (1, 2), (2, 4))
+
+
+def tile_list_rink_thickness_board_kernel(
+    tc, tab_words, tab_scales, offs, w1, page0, wgs, offs2, offs3, gs, lap, gx, w4_words, w4_scales, offs4, gb, out
+):
+    nc = tc.nc
+
+    def half_cols(h):
+        return slice(h * HALF, (h + 1) * HALF)
+
+    def list_half(tile, h):
+        return tile[:, h * LIST_COLS : (h + 1) * LIST_COLS]
+
+    def interleave(dst, src):
+        nc.scalar.copy(
+            out=dst.rearrange("p (c i t) -> p c t i", i=RUN, t=PACK),
+            in_=src.rearrange("p t (c i) -> p c t i", i=RUN),
+        )
+
+    with ExitStack() as ctx:
+        keep = ctx.enter_context(tc.tile_pool(name="keep", bufs=1))
+        psum = ctx.enter_context(tc.psum_pool(name="psum", bufs=1))
+
+        idx1 = keep.tile([P, S // 16], U16, name="idx1")
+        idx2 = keep.tile([P, S // 16], U16, name="idx2")
+        idx3 = keep.tile([P, NJ // 16], U16, name="idx3")
+        idx4 = keep.tile([P, NJ // 16], U16, name="idx4")
+        tab = [keep.tile([P, T], U32, name=f"tab{a}") for a in range(PASSES)]
+        tab_sc = keep.tile([P, T], U8, name="tab_sc")
+        page = [keep.tile([P, T2], F32, name=f"page{c}") for c in range(BLOCKS)]
+        lap_sb = [keep.tile([P, NJ], F32, name=f"lap{c}") for c in range(BLOCKS)]
+        wgs_sb = keep.tile([P, S], F32, name="wgs_sb", tag="wgs_sb")
+        gain_rows = keep.tile([P, P], F32, name="gain_rows")
+        gx_sb = keep.tile([P, PACK], F32, name="gx_sb")
+        w4_codes = keep.tile([P, 2 * H], U8, name="w4_codes", align_bytes=64)
+        w4_sc = keep.tile([P, H], U8, name="w4_sc", align_bytes=64)
+        ident = keep.tile([P, P], F32, name="ident")
+        w1_raw = {}
+        for g, (c0, c1) in enumerate(W1_GROUPS):
+            for a in range(PASSES):
+                w1_raw[g, a] = keep.tile([P, PACK, (c1 - c0) * P], F32, name=f"w1_raw{g}_{a}", tag=f"w1_raw{g}_{a}", align_bytes=64)
+
+        nc.gpsimd.memset(tab_sc[:].bitcast(I32), 0)
+        nc.gpsimd.memset(gain_rows[:], 0.0)
+        nc.gpsimd.memset(w4_sc[:].bitcast(I32), 0)
+        make_identity(nc, ident[:])
+
+        def load_tab(a):
+            nc.sync.dma_start(out=tab[a][:].bitcast(I32), in_=tab_words[a].rearrange("p n t -> p (n t)").bitcast(I32))
+
+        def load_w1(g, passes):
+            c0, c1 = W1_GROUPS[g]
+            for a in passes:
+                rows = w1[a * P * PACK : (a + 1) * P * PACK, c0 * P : c1 * P]
+                nc.sync.dma_start(out=w1_raw[g, a][:], in_=rows.rearrange("(p t) c -> p t c", t=PACK))
+
+        def load_rows(dst, src, c):
+            nc.sync.dma_start(out=dst[c][:], in_=src[c * P : (c + 1) * P, :])
+
+        nc.sync.dma_start(idx1[:], offs)
+        load_tab(0)
+        for q in range(4):
+            nc.sync.dma_start(
+                out=tab_sc[32 * q : 32 * q + 4 * PASSES, :].bitcast(I32),
+                in_=tab_scales[:, 4 * q : 4 * q + 4, :].bitcast(I32),
+            )
+        load_w1(0, [0])
+        load_tab(1)
+        load_w1(0, [1, 2])
+        load_tab(2)
+        nc.sync.dma_start(idx2[:], offs2)
+        load_rows(page, page0, 0)
+        nc.sync.dma_start(out=wgs_sb[:, half_cols(0)], in_=wgs[:, half_cols(0)])
+        load_w1(1, range(PASSES))
+        load_w1(2, [0])
+        nc.sync.dma_start(out=wgs_sb[:, half_cols(1)], in_=wgs[:, half_cols(1)])
+        load_w1(2, [1, 2])
+        load_rows(page, page0, 1)
+        nc.sync.dma_start(idx3[:], offs3)
+        load_rows(page, page0, 2)
+        nc.sync.dma_start(out=gain_rows[0:BLOCKS, :], in_=gs.rearrange("(c p) -> c p", p=P))
+        nc.sync.dma_start(out=gain_rows[BLOCKS : 2 * BLOCKS, :], in_=gb.rearrange("(c p) -> c p", p=P))
+        load_rows(lap_sb, lap, 0)
+        load_rows(lap_sb, lap, 1)
+        load_rows(page, page0, 3)
+        load_rows(lap_sb, lap, 2)
+        load_rows(lap_sb, lap, 3)
+        nc.sync.dma_start(out=gx_sb[:], in_=gx.rearrange("(p t) -> p t", t=PACK))
+        nc.sync.dma_start(out=w4_codes[:].bitcast(I32), in_=w4_words[0].bitcast(I32))
+        for q in range(4):
+            nc.sync.dma_start(
+                out=w4_sc[32 * q : 32 * q + 4, :].bitcast(I32), in_=w4_scales[0, 4 * q : 4 * q + 4, :].bitcast(I32)
+            )
+        nc.sync.dma_start(idx4[:], offs4)
+
+        v_sc = keep.tile([P, S], U8, name="v_sc", align_bytes=64)
+        v_codes = [keep.tile([P, S], U32, name=f"v_codes{a}", align_bytes=64) for a in range(PASSES)]
+        nc.vector.tensor_copy(v_sc[:], tab_sc[:].indirect(idx1[:]))
+        for a in range(PASSES - 1):
+            nc.vector.tensor_copy(v_codes[a][:], tab[a][:].indirect(idx1[:]))
+
+        w1_codes, w1_sc = {}, {}
+
+        def quantise_w1(g, slot):
+            c0, c1 = W1_GROUPS[g]
+            width = (c1 - c0) * P
+            codes = keep.tile([P, PASSES * width], U32, name=f"w1_codes{g}", tag=slot, align_bytes=64)
+            scales = keep.tile([P, PASSES * width], U8, name=f"w1_sc{g}", align_bytes=64)
+            for a in range(PASSES):
+                rounded = keep.tile([P, PACK * width], BF16, name=f"w1_bf{g}_{a}", align_bytes=64)
+                interleave(rounded[:], w1_raw[g, a][:])
+                cols = slice(a * width, (a + 1) * width)
+                nc.vector.quantize_mx(out=codes[:, cols].bitcast(FP8X4), scales=scales[:, cols], in_=rounded[:])
+                for c in range(c0, c1):
+                    block = slice(a * width + (c - c0) * P, a * width + (c - c0 + 1) * P)
+                    w1_codes[c, a] = codes[:, block]
+                    w1_sc[c, a] = scales[:, block]
+
+        def make_h(c, halves):
+            accs = [psum.tile([P, HALF], F32, name="acc", bufs=2) for h in range(HALVES)]
+            for a in range(PASSES):
+                for h in range(HALVES):
+                    nc.tensor.matmul_mx(
+                        out=accs[h][:],
+                        lhsT=w1_codes[c, a].bitcast(FP8X4),
+                        lhsT_scale=w1_sc[c, a],
+                        rhs=v_codes[a][:, half_cols(h)].bitcast(FP8X4),
+                        rhs_scale=v_sc[4 * a : P, half_cols(h)],
+                        start=(a == 0),
+                        stop=(a == PASSES - 1),
+                    )
+            for h in range(HALVES):
+                nc.scalar.copy(out=halves[h], in_=accs[h][:])
+
+        quantise_w1(0, "w1_codes0")
+        last = PASSES - 1
+        for h in range(HALVES):
+            nc.vector.tensor_copy(v_codes[last][:, half_cols(h)], tab[last][:].indirect(list_half(idx1, h)))
+        h_first = [keep.tile([P, HALF], F32, name=f"h0_{h}", tag=f"h0_{h}", align_bytes=64) for h in range(HALVES)]
+        make_h(0, [t[:] for t in h_first])
+        for h in range(HALVES):
+            nc.vector.tensor_tensor(page[0][:].indirect(list_half(idx2, h)), h_first[h][:], wgs_sb[:, half_cols(h)], MULT)
+        h_sb = {}
+
+        def make_h_whole(c, slot):
+            h_sb[c] = keep.tile([P, S], F32, name=f"h{c}", tag=slot, align_bytes=64)
+            make_h(c, [h_sb[c][:, half_cols(h)] for h in range(HALVES)])
+
+        def scatter(c):
+            nc.vector.tensor_tensor(page[c][:].indirect(idx2[:]), h_sb[c][:], wgs_sb[:], MULT)
+
+        quantise_w1(1, "h0_0")
+        quantise_w1(2, "h0_1")
+        make_h_whole(1, "w1_raw2_2")
+        scatter(1)
+        make_h_whole(2, "h2")
+        make_h_whole(3, "h3")
+
+        gains = keep.tile([P, 2 * BLOCKS], F32, name="gains", tag="h0_1", align_bytes=64)
+
+        gain_t = psum.tile([P, HALF], F32, name="z_t", bufs=2)
+        nc.tensor.transpose(gain_t[:, 0:P], gain_rows[:], ident[:])
+        nc.scalar.copy(out=gains[:], in_=gain_t[:, 0 : 2 * BLOCKS])
+
+        tanh_t = [keep.tile([P, HALF // P, PACK, P], F32, name=f"tanh_t{h}") for h in range(HALVES)]
+
+        def reread(c, pieces, slot):
+            picked = keep.tile([P, NJ], F32, name=f"picked{c}", tag=slot, align_bytes=64)
+            scaled = keep.tile([P, NJ], F32, name="scaled", bufs=2)
+            width = NJ // pieces
+            for u in range(pieces):
+                nc.vector.tensor_copy(
+                    picked[:, u * width : (u + 1) * width],
+                    page[c][:].indirect(idx3[:, u * width // 16 : (u + 1) * width // 16]),
+                )
+            for h in range(HALVES):
+                nc.scalar.activation(out=scaled[:, half_cols(h)], in_=picked[:, half_cols(h)], func=COPY, scale=gains[:, c : c + 1])
+                z_t = psum.tile([P, HALF], F32, name="z_t", bufs=2)
+                terms = (lap_sb[c], scaled)
+                for s, term in enumerate(terms):
+                    for b in range(HALF // P):
+                        nc.tensor.matmul(
+                            z_t[:, b * P : (b + 1) * P],
+                            lhsT=term[:, h * HALF + b * P : h * HALF + (b + 1) * P],
+                            rhs=ident[:],
+                            is_transpose=True,
+                            start=(s == 0 and b == 0),
+                            stop=(s == 1 and b == HALF // P - 1),
+                        )
+                nc.scalar.activation(
+                    out=tanh_t[h][:, :, :, 32 * c : 32 * (c + 1)],
+                    in_=z_t[:].rearrange("p (b q t) -> p b t q", t=PACK, q=32),
+                    func=TANH,
+                )
+
+        reread(0, 1, "picked0")
+        scatter(2)
+        reread(1, 1, "h2")
+        reread(2, 1, "picked0")
+        scatter(3)
+        reread(3, 2, "h3")
+
+        side_first = keep.tile([P, (BLOCKS - 1) * NJ], F32, name="side_first", tag="wgs_sb")
+        side = [side_first[:, c * NJ : (c + 1) * NJ] for c in range(BLOCKS - 1)]
+        for c in range(BLOCKS - 1):
+            nc.vector.tensor_copy(side[c], page[c][:].indirect(idx4[:]))
+
+        x_codes, x_sc = [], []
+
+        def quantise_x(h):
+            x_rows = keep.tile([P, PACK, HALF], BF16, name=f"x_rows{h}")
+            for t in range(PACK):
+                back = psum.tile([P, HALF], F32, name="back", bufs=4)
+                for b in range(HALF // P):
+                    nc.tensor.transpose(back[:, b * P : (b + 1) * P], tanh_t[h][:, b, t, :], ident[:])
+                nc.scalar.activation(out=x_rows[:, t, :], in_=back[:], func=COPY, scale=gx_sb[:, t : t + 1])
+            x_bf = keep.tile([P, PACK * HALF], BF16, name=f"x_bf{h}", tag=f"x_bf{h}", align_bytes=64)
+            interleave(x_bf[:], x_rows[:])
+            codes = keep.tile([P, HALF], U32, name=f"x_codes{h}", align_bytes=64)
+            scales = keep.tile([P, HALF], U8, name=f"x_sc{h}", align_bytes=64)
+            nc.vector.quantize_mx(out=codes[:].bitcast(FP8X4), scales=scales[:], in_=x_bf[:])
+            x_codes.append(codes)
+            x_sc.append(scales)
+
+        quantise_x(0)
+        side_last = keep.tile([P, NJ], F32, name="side_last", tag="x_bf0", align_bytes=64)
+        nc.vector.tensor_copy(side_last[:], page[BLOCKS - 1][:].indirect(idx4[:]))
+        side.append(side_last[:])
+        quantise_x(1)
+
+        results = {}
+
+        def weigh(h, c):
+            acc = psum.tile([P, HALF], F32, name="acc", bufs=2)
+            nc.tensor.matmul_mx(
+                out=acc[:],
+                lhsT=w4_codes[:, 2 * c * P : 2 * (c + 1) * P].bitcast(FP4X4),
+                lhsT_scale=w4_sc[:, c * P : (c + 1) * P],
+                rhs=x_codes[h][:].bitcast(FP8X4),
+                rhs_scale=x_sc[h][:],
+                start=True,
+                stop=True,
+            )
+            weighed = keep.tile([P, HALF], F32, name="weighed", bufs=3)
+            nc.vector.tensor_tensor(weighed[:], acc[:], lap_sb[c][:, half_cols(h)], MULT)
+            results[h, c] = weighed
+
+        def finish(h, c):
+            res = keep.tile([P, HALF], F32, name="res", bufs=4)
+            nc.vector.scalar_tensor_tensor(
+                out=res[:],
+                in0=side[c][:, half_cols(h)],
+                scalar=gains[:, BLOCKS + c : BLOCKS + c + 1],
+                in1=results[h, c][:],
+                op0=MULT,
+                op1=ADD,
+            )
+            nc.sync.dma_start(out=out[c * P : (c + 1) * P, half_cols(h)], in_=res[:])
+
+        steps = [(h, c) for h in range(HALVES) for c in range(BLOCKS)]
+        for i, step in enumerate(steps):
+            weigh(*step)
+            if i > 0:
+                finish(*steps[i - 1])
+        finish(*steps[-1])

@@ -25,6 +25,7 @@ PASSES = K // (P * PACK)
 BLOCKS = H // P
 HALF = 512
 HALVES = S // HALF
+QUARTER = HALF // 2
 LIST_COLS = HALF // 16
 RUN = 4
 W1_GROUPS = ((0, 1), (1, 2), (2, 4))
@@ -89,24 +90,23 @@ def tile_list_rink_thickness_board_kernel(
 
         nc.sync.dma_start(idx1[:], offs)
         load_tab(0)
+        load_w1(0, [0])
+        load_tab(1)
         for q in range(4):
             nc.sync.dma_start(
                 out=tab_sc[32 * q : 32 * q + 4 * PASSES, :].bitcast(I32),
                 in_=tab_scales[:, 4 * q : 4 * q + 4, :].bitcast(I32),
             )
-        load_w1(0, [0])
-        load_tab(1)
-        load_w1(0, [1, 2])
         load_tab(2)
+        load_w1(0, [1, 2])
         nc.sync.dma_start(idx2[:], offs2)
         load_rows(page, page0, 0)
         nc.sync.dma_start(out=wgs_sb[:, half_cols(0)], in_=wgs[:, half_cols(0)])
         load_w1(1, range(PASSES))
-        load_w1(2, [0])
         nc.sync.dma_start(out=wgs_sb[:, half_cols(1)], in_=wgs[:, half_cols(1)])
-        load_w1(2, [1, 2])
-        load_rows(page, page0, 1)
         nc.sync.dma_start(idx3[:], offs3)
+        load_rows(page, page0, 1)
+        load_w1(2, range(PASSES))
         load_rows(page, page0, 2)
         nc.sync.dma_start(out=gain_rows[0:BLOCKS, :], in_=gs.rearrange("(c p) -> c p", p=P))
         nc.sync.dma_start(out=gain_rows[BLOCKS : 2 * BLOCKS, :], in_=gb.rearrange("(c p) -> c p", p=P))
@@ -124,12 +124,28 @@ def tile_list_rink_thickness_board_kernel(
         nc.sync.dma_start(idx4[:], offs4)
 
         v_sc = keep.tile([P, S], U8, name="v_sc", align_bytes=64)
-        v_codes = [keep.tile([P, S], U32, name=f"v_codes{a}", align_bytes=64) for a in range(PASSES)]
+        v_first = keep.tile([P, S], U32, name="v_first", align_bytes=64)
+        v_codes = {(0, h): v_first[:, half_cols(h)] for h in range(HALVES)}
         nc.vector.tensor_copy(v_sc[:], tab_sc[:].indirect(idx1[:]))
-        for a in range(PASSES - 1):
-            nc.vector.tensor_copy(v_codes[a][:], tab[a][:].indirect(idx1[:]))
+        nc.vector.tensor_copy(v_first[:], tab[0][:].indirect(idx1[:]))
+
+        def gather_later_passes(h, slot):
+            words = keep.tile([P, (PASSES - 1) * HALF], U32, name=f"v_later{h}", tag=slot, align_bytes=64)
+            for a in range(1, PASSES):
+                v_codes[a, h] = words[:, half_cols(a - 1)]
+                nc.vector.tensor_copy(v_codes[a, h], tab[a][:].indirect(list_half(idx1, h)))
 
         w1_codes, w1_sc = {}, {}
+
+        w1_bf = {}
+
+        def round_w1(g, slot):
+            c0, c1 = W1_GROUPS[g]
+            width = PACK * (c1 - c0) * P
+            rounded = keep.tile([P, PASSES * width], BF16, name=f"w1_bf{g}", tag=slot, align_bytes=64)
+            for a in range(PASSES):
+                w1_bf[g, a] = rounded[:, a * width : (a + 1) * width]
+                interleave(w1_bf[g, a], w1_raw[g, a][:])
 
         def quantise_w1(g, slot):
             c0, c1 = W1_GROUPS[g]
@@ -137,10 +153,8 @@ def tile_list_rink_thickness_board_kernel(
             codes = keep.tile([P, PASSES * width], U32, name=f"w1_codes{g}", tag=slot, align_bytes=64)
             scales = keep.tile([P, PASSES * width], U8, name=f"w1_sc{g}", align_bytes=64)
             for a in range(PASSES):
-                rounded = keep.tile([P, PACK * width], BF16, name=f"w1_bf{g}_{a}", align_bytes=64)
-                interleave(rounded[:], w1_raw[g, a][:])
                 cols = slice(a * width, (a + 1) * width)
-                nc.vector.quantize_mx(out=codes[:, cols].bitcast(FP8X4), scales=scales[:, cols], in_=rounded[:])
+                nc.vector.quantize_mx(out=codes[:, cols].bitcast(FP8X4), scales=scales[:, cols], in_=w1_bf[g, a])
                 for c in range(c0, c1):
                     block = slice(a * width + (c - c0) * P, a * width + (c - c0 + 1) * P)
                     w1_codes[c, a] = codes[:, block]
@@ -154,7 +168,7 @@ def tile_list_rink_thickness_board_kernel(
                         out=accs[h][:],
                         lhsT=w1_codes[c, a].bitcast(FP8X4),
                         lhsT_scale=w1_sc[c, a],
-                        rhs=v_codes[a][:, half_cols(h)].bitcast(FP8X4),
+                        rhs=v_codes[a, h].bitcast(FP8X4),
                         rhs_scale=v_sc[4 * a : P, half_cols(h)],
                         start=(a == 0),
                         stop=(a == PASSES - 1),
@@ -162,11 +176,12 @@ def tile_list_rink_thickness_board_kernel(
             for h in range(HALVES):
                 nc.scalar.copy(out=halves[h], in_=accs[h][:])
 
+        gather_later_passes(0, "v_later0")
+        round_w1(0, "w1_bf0")
         quantise_w1(0, "w1_codes0")
-        last = PASSES - 1
-        for h in range(HALVES):
-            nc.vector.tensor_copy(v_codes[last][:, half_cols(h)], tab[last][:].indirect(list_half(idx1, h)))
-        h_first = [keep.tile([P, HALF], F32, name=f"h0_{h}", tag=f"h0_{h}", align_bytes=64) for h in range(HALVES)]
+        gather_later_passes(1, "w1_bf0")
+        round_w1(1, "w1_bf1")
+        h_first = [keep.tile([P, HALF], F32, name=f"h0_{h}", tag=slot, align_bytes=64) for h, slot in enumerate(("h0_0", "w1_raw1_2"))]
         make_h(0, [t[:] for t in h_first])
         for h in range(HALVES):
             nc.vector.tensor_tensor(page[0][:].indirect(list_half(idx2, h)), h_first[h][:], wgs_sb[:, half_cols(h)], MULT)
@@ -180,114 +195,136 @@ def tile_list_rink_thickness_board_kernel(
             nc.vector.tensor_tensor(page[c][:].indirect(idx2[:]), h_sb[c][:], wgs_sb[:], MULT)
 
         quantise_w1(1, "h0_0")
-        quantise_w1(2, "h0_1")
-        make_h_whole(1, "w1_raw2_2")
+        first_pick = keep.tile([P, HALF], F32, name="picked0_0", tag="picked0", align_bytes=64)
+        nc.vector.tensor_copy(first_pick[:], page[0][:].indirect(list_half(idx3, 0)))
+        make_h_whole(1, "h1")
         scatter(1)
+        round_w1(2, "h0_0")
+        quantise_w1(2, "h1")
         make_h_whole(2, "h2")
         make_h_whole(3, "h3")
 
-        gains = keep.tile([P, 2 * BLOCKS], F32, name="gains", tag="h0_1", align_bytes=64)
+        gains = keep.tile([P, 2 * BLOCKS], F32, name="gains", tag="h1", align_bytes=64)
 
         gain_t = psum.tile([P, HALF], F32, name="z_t", bufs=2)
         nc.tensor.transpose(gain_t[:, 0:P], gain_rows[:], ident[:])
         nc.scalar.copy(out=gains[:], in_=gain_t[:, 0 : 2 * BLOCKS])
 
-        tanh_t = [keep.tile([P, HALF // P, PACK, P], F32, name=f"tanh_t{h}") for h in range(HALVES)]
+        tanh_t = keep.tile([P, NJ // P, PACK, P], F32, name="tanh_t")
 
-        def reread(c, pieces, slot):
-            picked = keep.tile([P, NJ], F32, name=f"picked{c}", tag=slot, align_bytes=64)
-            scaled = keep.tile([P, NJ], F32, name="scaled", bufs=2)
-            width = NJ // pieces
-            for u in range(pieces):
-                nc.vector.tensor_copy(
-                    picked[:, u * width : (u + 1) * width],
-                    page[c][:].indirect(idx3[:, u * width // 16 : (u + 1) * width // 16]),
-                )
-            for h in range(HALVES):
-                nc.scalar.activation(out=scaled[:, half_cols(h)], in_=picked[:, half_cols(h)], func=COPY, scale=gains[:, c : c + 1])
-                z_t = psum.tile([P, HALF], F32, name="z_t", bufs=2)
-                terms = (lap_sb[c], scaled)
-                for s, term in enumerate(terms):
-                    for b in range(HALF // P):
-                        nc.tensor.matmul(
-                            z_t[:, b * P : (b + 1) * P],
-                            lhsT=term[:, h * HALF + b * P : h * HALF + (b + 1) * P],
-                            rhs=ident[:],
-                            is_transpose=True,
-                            start=(s == 0 and b == 0),
-                            stop=(s == 1 and b == HALF // P - 1),
-                        )
-                nc.scalar.activation(
-                    out=tanh_t[h][:, :, :, 32 * c : 32 * (c + 1)],
-                    in_=z_t[:].rearrange("p (b q t) -> p b t q", t=PACK, q=32),
-                    func=TANH,
-                )
+        def pick(c, first, width, dst):
+            nc.vector.tensor_copy(dst, page[c][:].indirect(idx3[:, first // 16 : (first + width) // 16]))
 
-        reread(0, 1, "picked0")
+        def squash(c, first, width, src):
+            scaled = keep.tile([P, HALF], F32, name="scaled", bufs=4)
+            nc.scalar.activation(out=scaled[:, 0:width], in_=src, func=COPY, scale=gains[:, c : c + 1])
+            z_t = psum.tile([P, HALF], F32, name="z_t", bufs=2)
+            terms = (lap_sb[c][:, first : first + width], scaled[:, 0:width])
+            for s, term in enumerate(terms):
+                for b in range(width // P):
+                    nc.tensor.matmul(
+                        z_t[:, b * P : (b + 1) * P],
+                        lhsT=term[:, b * P : (b + 1) * P],
+                        rhs=ident[:],
+                        is_transpose=True,
+                        start=(s == 0 and b == 0),
+                        stop=(s == 1 and b == width // P - 1),
+                    )
+            nc.scalar.activation(
+                out=tanh_t[:, first // P : (first + width) // P, :, 32 * c : 32 * (c + 1)],
+                in_=z_t[:, 0:width].rearrange("p (b q t) -> p b t q", t=PACK, q=32),
+                func=TANH,
+            )
+
+        held = keep.tile([P, HALF + NJ], F32, name="picked01", tag="h0_0", align_bytes=64)
+        pick(0, HALF, HALF, held[:, 0:HALF])
+        squash(0, 0, HALF, first_pick[:])
+        squash(0, HALF, HALF, held[:, 0:HALF])
+        pick(1, 0, NJ, held[:, HALF:])
+        for h in range(HALVES):
+            squash(1, h * HALF, HALF, held[:, half_cols(h + 1)])
         scatter(2)
-        reread(1, 1, "h2")
-        reread(2, 1, "picked0")
+        picked2 = keep.tile([P, NJ], F32, name="picked2")
+        pick(2, 0, NJ, picked2[:])
+        for h in range(HALVES):
+            squash(2, h * HALF, HALF, picked2[:, half_cols(h)])
         scatter(3)
-        reread(3, 2, "h3")
+        picked3 = keep.tile([P, NJ], F32, name="picked3")
+        for first, width in ((0, QUARTER), (QUARTER, QUARTER), (HALF, HALF)):
+            pick(3, first, width, picked3[:, first : first + width])
 
-        side_first = keep.tile([P, (BLOCKS - 1) * NJ], F32, name="side_first", tag="wgs_sb")
-        side = [side_first[:, c * NJ : (c + 1) * NJ] for c in range(BLOCKS - 1)]
+        side_first = keep.tile([P, BLOCKS * NJ - HALF], F32, name="side_first", tag="wgs_sb")
         for c in range(BLOCKS - 1):
-            nc.vector.tensor_copy(side[c], page[c][:].indirect(idx4[:]))
+            nc.vector.tensor_copy(side_first[:, c * NJ : (c + 1) * NJ], page[c][:].indirect(idx4[:]))
+        nc.vector.tensor_copy(side_first[:, 3 * NJ :], page[3][:].indirect(list_half(idx4, 0)))
 
-        x_codes, x_sc = [], []
+        def round_x(first, dst):
+            squash(3, first, QUARTER, picked3[:, first : first + QUARTER])
+            x_rows = keep.tile([P, PACK, QUARTER], BF16, name="x_rows", bufs=2)
+            for pair in range(PACK // 2):
+                back = psum.tile([P, 2, QUARTER], F32, name="back", bufs=4)
+                for e in range(2):
+                    t = 2 * pair + e
+                    for b in range(QUARTER // P):
+                        nc.tensor.transpose(back[:, e, b * P : (b + 1) * P], tanh_t[:, first // P + b, t, :], ident[:])
+                for e in range(2):
+                    t = 2 * pair + e
+                    nc.scalar.activation(out=x_rows[:, t, :], in_=back[:, e, :], func=COPY, scale=gx_sb[:, t : t + 1])
+            interleave(dst, x_rows[:])
 
-        def quantise_x(h):
-            x_rows = keep.tile([P, PACK, HALF], BF16, name=f"x_rows{h}")
-            for t in range(PACK):
-                back = psum.tile([P, HALF], F32, name="back", bufs=4)
-                for b in range(HALF // P):
-                    nc.tensor.transpose(back[:, b * P : (b + 1) * P], tanh_t[h][:, b, t, :], ident[:])
-                nc.scalar.activation(out=x_rows[:, t, :], in_=back[:], func=COPY, scale=gx_sb[:, t : t + 1])
-            x_bf = keep.tile([P, PACK * HALF], BF16, name=f"x_bf{h}", tag=f"x_bf{h}", align_bytes=64)
-            interleave(x_bf[:], x_rows[:])
-            codes = keep.tile([P, HALF], U32, name=f"x_codes{h}", align_bytes=64)
-            scales = keep.tile([P, HALF], U8, name=f"x_sc{h}", align_bytes=64)
-            nc.vector.quantize_mx(out=codes[:].bitcast(FP8X4), scales=scales[:], in_=x_bf[:])
-            x_codes.append(codes)
-            x_sc.append(scales)
+        x_codes = keep.tile([P, NJ], U32, name="x_codes", align_bytes=64)
+        x_sc = keep.tile([P, NJ], U8, name="x_sc", align_bytes=64)
 
-        quantise_x(0)
-        side_last = keep.tile([P, NJ], F32, name="side_last", tag="x_bf0", align_bytes=64)
-        nc.vector.tensor_copy(side_last[:], page[BLOCKS - 1][:].indirect(idx4[:]))
-        side.append(side_last[:])
-        quantise_x(1)
+        def quantise_x(first, width):
+            x_bf = keep.tile([P, PACK * width], BF16, name=f"x_bf{first}", tag=f"x_bf{first}", align_bytes=64)
+            for u in range(width // QUARTER):
+                round_x(first + u * QUARTER, x_bf[:, u * PACK * QUARTER : (u + 1) * PACK * QUARTER])
+            cols = slice(first, first + width)
+            nc.vector.quantize_mx(out=x_codes[:, cols].bitcast(FP8X4), scales=x_sc[:, cols], in_=x_bf[:])
+
+        chunks = ((0, HALF), (HALF, QUARTER), (HALF + QUARTER, QUARTER))
+        quantise_x(*chunks[0])
+        side_last = keep.tile([P, HALF], F32, name="side_last", tag="x_bf0", align_bytes=64)
+        nc.vector.tensor_copy(side_last[:], page[3][:].indirect(list_half(idx4, 1)))
+        for chunk in chunks[1:]:
+            quantise_x(*chunk)
+
+        def side(c, first, width):
+            if c == 3 and first >= HALF:
+                return side_last[:, first - HALF : first - HALF + width]
+            return side_first[:, c * NJ + first : c * NJ + first + width]
 
         results = {}
 
-        def weigh(h, c):
+        def weigh(first, width, c):
+            cols = slice(first, first + width)
             acc = psum.tile([P, HALF], F32, name="acc", bufs=2)
             nc.tensor.matmul_mx(
-                out=acc[:],
+                out=acc[:, 0:width],
                 lhsT=w4_codes[:, 2 * c * P : 2 * (c + 1) * P].bitcast(FP4X4),
                 lhsT_scale=w4_sc[:, c * P : (c + 1) * P],
-                rhs=x_codes[h][:].bitcast(FP8X4),
-                rhs_scale=x_sc[h][:],
+                rhs=x_codes[:, cols].bitcast(FP8X4),
+                rhs_scale=x_sc[:, cols],
                 start=True,
                 stop=True,
             )
             weighed = keep.tile([P, HALF], F32, name="weighed", bufs=3)
-            nc.vector.tensor_tensor(weighed[:], acc[:], lap_sb[c][:, half_cols(h)], MULT)
-            results[h, c] = weighed
+            nc.vector.tensor_tensor(weighed[:, 0:width], acc[:, 0:width], lap_sb[c][:, cols], MULT)
+            results[first, c] = weighed
 
-        def finish(h, c):
-            res = keep.tile([P, HALF], F32, name="res", bufs=4)
+        def finish(first, width, c):
+            res = keep.tile([P, HALF], F32, name="res", bufs=6)
             nc.vector.scalar_tensor_tensor(
-                out=res[:],
-                in0=side[c][:, half_cols(h)],
+                out=res[:, 0:width],
+                in0=side(c, first, width),
                 scalar=gains[:, BLOCKS + c : BLOCKS + c + 1],
-                in1=results[h, c][:],
+                in1=results[first, c][:, 0:width],
                 op0=MULT,
                 op1=ADD,
             )
-            nc.sync.dma_start(out=out[c * P : (c + 1) * P, half_cols(h)], in_=res[:])
+            nc.sync.dma_start(out=out[c * P : (c + 1) * P, first : first + width], in_=res[:, 0:width])
 
-        steps = [(h, c) for h in range(HALVES) for c in range(BLOCKS)]
+        steps = [(first, width, c) for first, width in chunks for c in range(BLOCKS)]
         for i, step in enumerate(steps):
             weigh(*step)
             if i > 0:

@@ -23,12 +23,17 @@ P = 128
 PACK = 4
 PASSES = K // (P * PACK)
 BLOCKS = H // P
+LAST = BLOCKS - 1
+QUADRANT = 32
+SCALE_ROWS = 4
+PER_COLUMN = 16
 HALF = 512
 HALVES = S // HALF
 QUARTER = HALF // 2
-LIST_COLS = HALF // 16
 RUN = 4
 W1_GROUPS = ((0, 1), (1, 2), (2, 4))
+PASS_RUNS = ((0, 1), (1, 3))
+X_CHUNKS = ((0, HALF), (HALF, QUARTER), (HALF + QUARTER, QUARTER))
 
 
 def tile_list_rink_thickness_board_kernel(
@@ -39,8 +44,8 @@ def tile_list_rink_thickness_board_kernel(
     def half_cols(h):
         return slice(h * HALF, (h + 1) * HALF)
 
-    def list_half(tile, h):
-        return tile[:, h * LIST_COLS : (h + 1) * LIST_COLS]
+    def entries(list_tile, first, count):
+        return list_tile[:, first // PER_COLUMN : (first + count) // PER_COLUMN]
 
     def interleave(dst, src):
         nc.scalar.copy(
@@ -52,14 +57,14 @@ def tile_list_rink_thickness_board_kernel(
         keep = ctx.enter_context(tc.tile_pool(name="keep", bufs=1))
         psum = ctx.enter_context(tc.psum_pool(name="psum", bufs=1))
 
-        idx1 = keep.tile([P, S // 16], U16, name="idx1")
-        idx2 = keep.tile([P, S // 16], U16, name="idx2")
-        idx3 = keep.tile([P, NJ // 16], U16, name="idx3")
-        idx4 = keep.tile([P, NJ // 16], U16, name="idx4")
+        idx1 = keep.tile([P, S // PER_COLUMN], U16, name="idx1")
+        idx2 = keep.tile([P, S // PER_COLUMN], U16, name="idx2")
+        idx3 = keep.tile([P, NJ // PER_COLUMN], U16, name="idx3")
+        idx4 = keep.tile([P, NJ // PER_COLUMN], U16, name="idx4")
         tab = [keep.tile([P, T], U32, name=f"tab{a}") for a in range(PASSES)]
         tab_sc = keep.tile([P, T], U8, name="tab_sc")
         page = [keep.tile([P, T2], F32, name=f"page{c}") for c in range(BLOCKS)]
-        lap_sb = [keep.tile([P, NJ], F32, name=f"lap{c}") for c in range(BLOCKS)]
+        lap_sb = keep.tile([P, BLOCKS, NJ], F32, name="lap_sb")
         wgs_sb = keep.tile([P, S], F32, name="wgs_sb", tag="wgs_sb")
         gain_rows = keep.tile([P, P], F32, name="gain_rows")
         gx_sb = keep.tile([P, PACK], F32, name="gx_sb")
@@ -69,7 +74,8 @@ def tile_list_rink_thickness_board_kernel(
         w1_raw = {}
         for g, (c0, c1) in enumerate(W1_GROUPS):
             for a in range(PASSES):
-                w1_raw[g, a] = keep.tile([P, PACK, (c1 - c0) * P], F32, name=f"w1_raw{g}_{a}", tag=f"w1_raw{g}_{a}", align_bytes=64)
+                tag = f"w1_raw{g}_{a}"
+                w1_raw[g, a] = keep.tile([P, PACK, (c1 - c0) * P], F32, name=tag, tag=tag, align_bytes=64)
 
         nc.gpsimd.memset(tab_sc[:].bitcast(I32), 0)
         nc.gpsimd.memset(gain_rows[:], 0.0)
@@ -85,41 +91,48 @@ def tile_list_rink_thickness_board_kernel(
                 rows = w1[a * P * PACK : (a + 1) * P * PACK, c0 * P : c1 * P]
                 nc.sync.dma_start(out=w1_raw[g, a][:], in_=rows.rearrange("(p t) c -> p t c", t=PACK))
 
-        def load_rows(dst, src, c):
-            nc.sync.dma_start(out=dst[c][:], in_=src[c * P : (c + 1) * P, :])
+        def load_page(c):
+            nc.sync.dma_start(out=page[c][:], in_=page0[c * P : (c + 1) * P, :])
 
-        nc.sync.dma_start(idx1[:], offs)
+        def load_lap(c):
+            nc.sync.dma_start(out=lap_sb[:, c, :], in_=lap[c * P : (c + 1) * P, :])
+
+        def load_wgs(h):
+            nc.sync.dma_start(out=wgs_sb[:, half_cols(h)], in_=wgs[:, half_cols(h)])
+
         load_tab(0)
+        nc.sync.dma_start(idx1[:], offs)
         load_w1(0, [0])
         load_tab(1)
-        for q in range(4):
+        for q in range(P // QUADRANT):
             nc.sync.dma_start(
-                out=tab_sc[32 * q : 32 * q + 4 * PASSES, :].bitcast(I32),
-                in_=tab_scales[:, 4 * q : 4 * q + 4, :].bitcast(I32),
+                out=tab_sc[QUADRANT * q : QUADRANT * q + SCALE_ROWS * PASSES, :].bitcast(I32),
+                in_=tab_scales[:, SCALE_ROWS * q : SCALE_ROWS * (q + 1), :].bitcast(I32),
             )
         load_tab(2)
         load_w1(0, [1, 2])
         nc.sync.dma_start(idx2[:], offs2)
-        load_rows(page, page0, 0)
-        nc.sync.dma_start(out=wgs_sb[:, half_cols(0)], in_=wgs[:, half_cols(0)])
+        load_page(0)
+        load_wgs(0)
         load_w1(1, range(PASSES))
-        nc.sync.dma_start(out=wgs_sb[:, half_cols(1)], in_=wgs[:, half_cols(1)])
+        load_wgs(1)
         nc.sync.dma_start(idx3[:], offs3)
-        load_rows(page, page0, 1)
+        load_page(1)
         load_w1(2, range(PASSES))
-        load_rows(page, page0, 2)
+        load_page(2)
         nc.sync.dma_start(out=gain_rows[0:BLOCKS, :], in_=gs.rearrange("(c p) -> c p", p=P))
         nc.sync.dma_start(out=gain_rows[BLOCKS : 2 * BLOCKS, :], in_=gb.rearrange("(c p) -> c p", p=P))
-        load_rows(lap_sb, lap, 0)
-        load_rows(lap_sb, lap, 1)
-        load_rows(page, page0, 3)
-        load_rows(lap_sb, lap, 2)
-        load_rows(lap_sb, lap, 3)
+        load_lap(0)
+        load_lap(1)
+        load_page(3)
+        load_lap(2)
+        load_lap(3)
         nc.sync.dma_start(out=gx_sb[:], in_=gx.rearrange("(p t) -> p t", t=PACK))
         nc.sync.dma_start(out=w4_codes[:].bitcast(I32), in_=w4_words[0].bitcast(I32))
-        for q in range(4):
+        for q in range(P // QUADRANT):
             nc.sync.dma_start(
-                out=w4_sc[32 * q : 32 * q + 4, :].bitcast(I32), in_=w4_scales[0, 4 * q : 4 * q + 4, :].bitcast(I32)
+                out=w4_sc[QUADRANT * q : QUADRANT * q + SCALE_ROWS, :].bitcast(I32),
+                in_=w4_scales[0, SCALE_ROWS * q : SCALE_ROWS * (q + 1), :].bitcast(I32),
             )
         nc.sync.dma_start(idx4[:], offs4)
 
@@ -129,97 +142,102 @@ def tile_list_rink_thickness_board_kernel(
         nc.vector.tensor_copy(v_sc[:], tab_sc[:].indirect(idx1[:]))
         nc.vector.tensor_copy(v_first[:], tab[0][:].indirect(idx1[:]))
 
-        def gather_later_passes(h, slot):
-            words = keep.tile([P, (PASSES - 1) * HALF], U32, name=f"v_later{h}", tag=slot, align_bytes=64)
+        def gather_later_passes(h, tag):
+            words = keep.tile([P, (PASSES - 1) * HALF], U32, name=f"v_later{h}", tag=tag, align_bytes=64)
             for a in range(1, PASSES):
                 v_codes[a, h] = words[:, half_cols(a - 1)]
-                nc.vector.tensor_copy(v_codes[a, h], tab[a][:].indirect(list_half(idx1, h)))
+                nc.vector.tensor_copy(v_codes[a, h], tab[a][:].indirect(entries(idx1, h * HALF, HALF)))
 
-        w1_codes, w1_sc = {}, {}
+        w1_bf, w1_codes, w1_sc = {}, {}, {}
 
-        w1_bf = {}
-
-        def round_w1(g, slot):
+        def round_w1(g, tag):
             c0, c1 = W1_GROUPS[g]
             width = PACK * (c1 - c0) * P
-            rounded = keep.tile([P, PASSES * width], BF16, name=f"w1_bf{g}", tag=slot, align_bytes=64)
+            w1_bf[g] = keep.tile([P, PASSES * width], BF16, name=f"w1_bf{g}", tag=tag, align_bytes=64)
             for a in range(PASSES):
-                w1_bf[g, a] = rounded[:, a * width : (a + 1) * width]
-                interleave(w1_bf[g, a], w1_raw[g, a][:])
+                interleave(w1_bf[g][:, a * width : (a + 1) * width], w1_raw[g, a][:])
 
-        def quantise_w1(g, slot):
+        def quantise_w1(g, tag):
             c0, c1 = W1_GROUPS[g]
             width = (c1 - c0) * P
-            codes = keep.tile([P, PASSES * width], U32, name=f"w1_codes{g}", tag=slot, align_bytes=64)
+            codes = keep.tile([P, PASSES * width], U32, name=f"w1_codes{g}", tag=tag, align_bytes=64)
             scales = keep.tile([P, PASSES * width], U8, name=f"w1_sc{g}", align_bytes=64)
+            for a0, a1 in PASS_RUNS:
+                nc.vector.quantize_mx(
+                    out=codes[:, a0 * width : a1 * width].bitcast(FP8X4),
+                    scales=scales[:, a0 * width : a1 * width],
+                    in_=w1_bf[g][:, PACK * a0 * width : PACK * a1 * width],
+                )
             for a in range(PASSES):
-                cols = slice(a * width, (a + 1) * width)
-                nc.vector.quantize_mx(out=codes[:, cols].bitcast(FP8X4), scales=scales[:, cols], in_=w1_bf[g, a])
                 for c in range(c0, c1):
-                    block = slice(a * width + (c - c0) * P, a * width + (c - c0 + 1) * P)
-                    w1_codes[c, a] = codes[:, block]
-                    w1_sc[c, a] = scales[:, block]
+                    cols = slice(a * width + (c - c0) * P, a * width + (c - c0 + 1) * P)
+                    w1_codes[c, a] = codes[:, cols]
+                    w1_sc[c, a] = scales[:, cols]
 
         def make_h(c, halves):
-            accs = [psum.tile([P, HALF], F32, name="acc", bufs=2) for h in range(HALVES)]
+            banks = [psum.tile([P, HALF], F32, name="acc", tag="acc", bufs=2) for h in range(HALVES)]
             for a in range(PASSES):
                 for h in range(HALVES):
                     nc.tensor.matmul_mx(
-                        out=accs[h][:],
+                        out=banks[h][:],
                         lhsT=w1_codes[c, a].bitcast(FP8X4),
                         lhsT_scale=w1_sc[c, a],
                         rhs=v_codes[a, h].bitcast(FP8X4),
-                        rhs_scale=v_sc[4 * a : P, half_cols(h)],
+                        rhs_scale=v_sc[SCALE_ROWS * a : P, half_cols(h)],
                         start=(a == 0),
                         stop=(a == PASSES - 1),
                     )
             for h in range(HALVES):
-                nc.scalar.copy(out=halves[h], in_=accs[h][:])
+                nc.scalar.copy(out=halves[h], in_=banks[h][:])
 
         gather_later_passes(0, "v_later0")
         round_w1(0, "w1_bf0")
         quantise_w1(0, "w1_codes0")
         gather_later_passes(1, "w1_bf0")
         round_w1(1, "w1_bf1")
-        h_first = [keep.tile([P, HALF], F32, name=f"h0_{h}", tag=slot, align_bytes=64) for h, slot in enumerate(("h0_0", "w1_raw1_2"))]
-        make_h(0, [t[:] for t in h_first])
+        h_first = [
+            keep.tile([P, HALF], F32, name=f"h0_{h}", tag=tag, align_bytes=64)
+            for h, tag in enumerate(("h0_0", "w1_raw1_2"))
+        ]
+        make_h(0, [tile[:] for tile in h_first])
         for h in range(HALVES):
-            nc.vector.tensor_tensor(page[0][:].indirect(list_half(idx2, h)), h_first[h][:], wgs_sb[:, half_cols(h)], MULT)
+            window = page[0][:].indirect(entries(idx2, h * HALF, HALF))
+            nc.vector.tensor_tensor(window, h_first[h][:], wgs_sb[:, half_cols(h)], MULT)
+
         h_sb = {}
 
-        def make_h_whole(c, slot):
-            h_sb[c] = keep.tile([P, S], F32, name=f"h{c}", tag=slot, align_bytes=64)
+        def make_h_whole(c):
+            h_sb[c] = keep.tile([P, S], F32, name=f"h{c}", tag=f"h{c}", align_bytes=64)
             make_h(c, [h_sb[c][:, half_cols(h)] for h in range(HALVES)])
 
         def scatter(c):
             nc.vector.tensor_tensor(page[c][:].indirect(idx2[:]), h_sb[c][:], wgs_sb[:], MULT)
 
+        def pick(c, first, width, dst):
+            nc.vector.tensor_copy(dst, page[c][:].indirect(entries(idx3, first, width)))
+
         quantise_w1(1, "h0_0")
-        first_pick = keep.tile([P, HALF], F32, name="picked0_0", tag="picked0", align_bytes=64)
-        nc.vector.tensor_copy(first_pick[:], page[0][:].indirect(list_half(idx3, 0)))
-        make_h_whole(1, "h1")
+        first_pick = keep.tile([P, HALF], F32, name="first_pick", align_bytes=64)
+        pick(0, 0, HALF, first_pick[:])
+        make_h_whole(1)
         scatter(1)
         round_w1(2, "h0_0")
         quantise_w1(2, "h1")
-        make_h_whole(2, "h2")
-        make_h_whole(3, "h3")
+        make_h_whole(2)
+        make_h_whole(3)
 
         gains = keep.tile([P, 2 * BLOCKS], F32, name="gains", tag="h1", align_bytes=64)
-
         gain_t = psum.tile([P, HALF], F32, name="z_t", bufs=2)
         nc.tensor.transpose(gain_t[:, 0:P], gain_rows[:], ident[:])
         nc.scalar.copy(out=gains[:], in_=gain_t[:, 0 : 2 * BLOCKS])
 
         tanh_t = keep.tile([P, NJ // P, PACK, P], F32, name="tanh_t")
 
-        def pick(c, first, width, dst):
-            nc.vector.tensor_copy(dst, page[c][:].indirect(idx3[:, first // 16 : (first + width) // 16]))
-
         def squash(c, first, width, src):
             scaled = keep.tile([P, HALF], F32, name="scaled", bufs=4)
             nc.scalar.activation(out=scaled[:, 0:width], in_=src, func=COPY, scale=gains[:, c : c + 1])
             z_t = psum.tile([P, HALF], F32, name="z_t", bufs=2)
-            terms = (lap_sb[c][:, first : first + width], scaled[:, 0:width])
+            terms = (lap_sb[:, c, first : first + width], scaled[:, 0:width])
             for s, term in enumerate(terms):
                 for b in range(width // P):
                     nc.tensor.matmul(
@@ -228,47 +246,48 @@ def tile_list_rink_thickness_board_kernel(
                         rhs=ident[:],
                         is_transpose=True,
                         start=(s == 0 and b == 0),
-                        stop=(s == 1 and b == width // P - 1),
+                        stop=(s == len(terms) - 1 and b == width // P - 1),
                     )
+            per_block = P // PACK
             nc.scalar.activation(
-                out=tanh_t[:, first // P : (first + width) // P, :, 32 * c : 32 * (c + 1)],
-                in_=z_t[:, 0:width].rearrange("p (b q t) -> p b t q", t=PACK, q=32),
+                out=tanh_t[:, first // P : (first + width) // P, :, per_block * c : per_block * (c + 1)],
+                in_=z_t[:, 0:width].rearrange("p (b q t) -> p b t q", t=PACK, q=per_block),
                 func=TANH,
             )
 
-        held = keep.tile([P, HALF + NJ], F32, name="picked01", tag="h0_0", align_bytes=64)
-        pick(0, HALF, HALF, held[:, 0:HALF])
+        later_picks = keep.tile([P, HALF + NJ], F32, name="later_picks", tag="h0_0", align_bytes=64)
+        pick(0, HALF, HALF, later_picks[:, 0:HALF])
         squash(0, 0, HALF, first_pick[:])
-        squash(0, HALF, HALF, held[:, 0:HALF])
-        pick(1, 0, NJ, held[:, HALF:])
+        squash(0, HALF, HALF, later_picks[:, 0:HALF])
+        pick(1, 0, NJ, later_picks[:, HALF:])
         for h in range(HALVES):
-            squash(1, h * HALF, HALF, held[:, half_cols(h + 1)])
+            squash(1, h * HALF, HALF, later_picks[:, half_cols(h + 1)])
         scatter(2)
         picked2 = keep.tile([P, NJ], F32, name="picked2")
         pick(2, 0, NJ, picked2[:])
         for h in range(HALVES):
             squash(2, h * HALF, HALF, picked2[:, half_cols(h)])
-        scatter(3)
-        picked3 = keep.tile([P, NJ], F32, name="picked3")
+        scatter(LAST)
+        picked_last = keep.tile([P, NJ], F32, name="picked_last")
         for first, width in ((0, QUARTER), (QUARTER, QUARTER), (HALF, HALF)):
-            pick(3, first, width, picked3[:, first : first + width])
+            pick(LAST, first, width, picked_last[:, first : first + width])
 
         side_first = keep.tile([P, BLOCKS * NJ - HALF], F32, name="side_first", tag="wgs_sb")
-        for c in range(BLOCKS - 1):
+        for c in range(LAST):
             nc.vector.tensor_copy(side_first[:, c * NJ : (c + 1) * NJ], page[c][:].indirect(idx4[:]))
-        nc.vector.tensor_copy(side_first[:, 3 * NJ :], page[3][:].indirect(list_half(idx4, 0)))
+        nc.vector.tensor_copy(side_first[:, LAST * NJ :], page[LAST][:].indirect(entries(idx4, 0, HALF)))
 
         def round_x(first, dst):
-            squash(3, first, QUARTER, picked3[:, first : first + QUARTER])
+            squash(LAST, first, QUARTER, picked_last[:, first : first + QUARTER])
             x_rows = keep.tile([P, PACK, QUARTER], BF16, name="x_rows", bufs=2)
-            for pair in range(PACK // 2):
-                back = psum.tile([P, 2, QUARTER], F32, name="back", bufs=4)
-                for e in range(2):
-                    t = 2 * pair + e
+            per_bank = HALF // QUARTER
+            for t0 in range(0, PACK, per_bank):
+                back = psum.tile([P, per_bank, QUARTER], F32, name="back", bufs=4)
+                for e in range(per_bank):
                     for b in range(QUARTER // P):
-                        nc.tensor.transpose(back[:, e, b * P : (b + 1) * P], tanh_t[:, first // P + b, t, :], ident[:])
-                for e in range(2):
-                    t = 2 * pair + e
+                        nc.tensor.transpose(back[:, e, b * P : (b + 1) * P], tanh_t[:, first // P + b, t0 + e, :], ident[:])
+                for e in range(per_bank):
+                    t = t0 + e
                     nc.scalar.activation(out=x_rows[:, t, :], in_=back[:, e, :], func=COPY, scale=gx_sb[:, t : t + 1])
             interleave(dst, x_rows[:])
 
@@ -282,49 +301,58 @@ def tile_list_rink_thickness_board_kernel(
             cols = slice(first, first + width)
             nc.vector.quantize_mx(out=x_codes[:, cols].bitcast(FP8X4), scales=x_sc[:, cols], in_=x_bf[:])
 
-        chunks = ((0, HALF), (HALF, QUARTER), (HALF + QUARTER, QUARTER))
-        quantise_x(*chunks[0])
+        quantise_x(*X_CHUNKS[0])
         side_last = keep.tile([P, HALF], F32, name="side_last", tag="x_bf0", align_bytes=64)
-        nc.vector.tensor_copy(side_last[:], page[3][:].indirect(list_half(idx4, 1)))
-        for chunk in chunks[1:]:
+        nc.vector.tensor_copy(side_last[:], page[LAST][:].indirect(entries(idx4, HALF, HALF)))
+        for chunk in X_CHUNKS[1:]:
             quantise_x(*chunk)
 
         def side(c, first, width):
-            if c == 3 and first >= HALF:
+            if c == LAST and first >= HALF:
                 return side_last[:, first - HALF : first - HALF + width]
             return side_first[:, c * NJ + first : c * NJ + first + width]
 
-        results = {}
+        weighed = {}
 
-        def weigh(first, width, c):
+        def weigh(first, width, c0):
             cols = slice(first, first + width)
-            acc = psum.tile([P, HALF], F32, name="acc", bufs=2)
-            nc.tensor.matmul_mx(
-                out=acc[:, 0:width],
-                lhsT=w4_codes[:, 2 * c * P : 2 * (c + 1) * P].bitcast(FP4X4),
-                lhsT_scale=w4_sc[:, c * P : (c + 1) * P],
-                rhs=x_codes[:, cols].bitcast(FP8X4),
-                rhs_scale=x_sc[:, cols],
-                start=True,
-                stop=True,
+            count = HALF // width
+            bank = psum.tile([P, HALF], F32, name="y", tag="acc", bufs=2)
+            for e in range(count):
+                c = c0 + e
+                nc.tensor.matmul_mx(
+                    out=bank[:, e * width : (e + 1) * width],
+                    lhsT=w4_codes[:, 2 * c * P : 2 * (c + 1) * P].bitcast(FP4X4),
+                    lhsT_scale=w4_sc[:, c * P : (c + 1) * P],
+                    rhs=x_codes[:, cols].bitcast(FP8X4),
+                    rhs_scale=x_sc[:, cols],
+                    start=True,
+                    stop=True,
+                )
+            product = keep.tile([P, HALF], F32, name="product", bufs=3)
+            nc.vector.tensor_tensor(
+                product[:].rearrange("p (e j) -> p e j", e=count),
+                bank[:].rearrange("p (e j) -> p e j", e=count),
+                lap_sb[:, c0 : c0 + count, cols],
+                MULT,
             )
-            weighed = keep.tile([P, HALF], F32, name="weighed", bufs=3)
-            nc.vector.tensor_tensor(weighed[:, 0:width], acc[:, 0:width], lap_sb[c][:, cols], MULT)
-            results[first, c] = weighed
+            for e in range(count):
+                weighed[first, c0 + e] = product[:, e * width : (e + 1) * width]
 
-        def finish(first, width, c):
-            res = keep.tile([P, HALF], F32, name="res", bufs=6)
-            nc.vector.scalar_tensor_tensor(
-                out=res[:, 0:width],
-                in0=side(c, first, width),
-                scalar=gains[:, BLOCKS + c : BLOCKS + c + 1],
-                in1=results[first, c][:, 0:width],
-                op0=MULT,
-                op1=ADD,
-            )
-            nc.sync.dma_start(out=out[c * P : (c + 1) * P, first : first + width], in_=res[:, 0:width])
+        def finish(first, width, c0):
+            for c in range(c0, c0 + HALF // width):
+                res = keep.tile([P, HALF], F32, name="res", bufs=6)
+                nc.vector.scalar_tensor_tensor(
+                    out=res[:, 0:width],
+                    in0=side(c, first, width),
+                    scalar=gains[:, BLOCKS + c : BLOCKS + c + 1],
+                    in1=weighed[first, c],
+                    op0=MULT,
+                    op1=ADD,
+                )
+                nc.sync.dma_start(out=out[c * P : (c + 1) * P, first : first + width], in_=res[:, 0:width])
 
-        steps = [(first, width, c) for first, width in chunks for c in range(BLOCKS)]
+        steps = [(first, width, c0) for first, width in X_CHUNKS for c0 in range(0, BLOCKS, HALF // width)]
         for i, step in enumerate(steps):
             weigh(*step)
             if i > 0:

from contextlib import ExitStack

import concourse.mybir as mybir
from concourse.masks import make_identity

K, H, T, S, T2, NJ = 1536, 512, 2048, 1024, 2048, 1024
FLOPS = 2 * K * H * S + 2 * H * H * NJ

F32 = mybir.dt.float32
BF16 = mybir.dt.bfloat16
I32 = mybir.dt.int32
U32 = mybir.dt.uint32
U16 = mybir.dt.uint16
U8 = mybir.dt.uint8
FP8X4 = mybir.dt.float8_e4m3fn_x4
FP4X4 = mybir.dt.float4_e2m1fn_x4
MULT = mybir.AluOpType.mult
ADD = mybir.AluOpType.add
COPY = mybir.ActivationFunctionType.Copy
TANH = mybir.ActivationFunctionType.Tanh

P = 128
PACK = 4
PASSES = K // (P * PACK)
BLOCKS = H // P
LAST = BLOCKS - 1
QUADRANT = 32
SCALE_ROWS = 4
PER_COLUMN = 16
HALF = 512
HALVES = S // HALF
QUARTER = HALF // 2
RUN = 4
W1_GROUPS = ((0, 1), (1, 2), (2, 4))
PASS_RUNS = ((0, 1), (1, 3))
X_CHUNKS = ((0, HALF), (HALF, QUARTER), (HALF + QUARTER, QUARTER))


def tile_list_rink_thickness_board_kernel(
    tc, tab_words, tab_scales, offs, w1, page0, wgs, offs2, offs3, gs, lap, gx, w4_words, w4_scales, offs4, gb, out
):
    nc = tc.nc

    def half_cols(h):
        return slice(h * HALF, (h + 1) * HALF)

    def entries(list_tile, first, count):
        return list_tile[:, first // PER_COLUMN : (first + count) // PER_COLUMN]

    def interleave(dst, src):
        nc.scalar.copy(
            out=dst.rearrange("p (c i t) -> p c t i", i=RUN, t=PACK),
            in_=src.rearrange("p t (c i) -> p c t i", i=RUN),
        )

    with ExitStack() as ctx:
        keep = ctx.enter_context(tc.tile_pool(name="keep", bufs=1))
        psum = ctx.enter_context(tc.psum_pool(name="psum", bufs=1))

        idx1 = keep.tile([P, S // PER_COLUMN], U16, name="idx1")
        idx2 = keep.tile([P, S // PER_COLUMN], U16, name="idx2")
        idx3 = keep.tile([P, NJ // PER_COLUMN], U16, name="idx3")
        idx4 = keep.tile([P, NJ // PER_COLUMN], U16, name="idx4")
        tab = [keep.tile([P, T], U32, name=f"tab{a}") for a in range(PASSES)]
        tab_sc = keep.tile([P, T], U8, name="tab_sc")
        page = [keep.tile([P, T2], F32, name=f"page{c}") for c in range(BLOCKS)]
        lap_sb = keep.tile([P, BLOCKS, NJ], F32, name="lap_sb")
        wgs_sb = keep.tile([P, S], F32, name="wgs_sb", tag="wgs_sb")
        gain_rows = keep.tile([P, P], F32, name="gain_rows")
        gx_sb = keep.tile([P, PACK], F32, name="gx_sb")
        w4_codes = keep.tile([P, 2 * H], U8, name="w4_codes", align_bytes=64)
        w4_sc = keep.tile([P, H], U8, name="w4_sc", align_bytes=64)
        ident = keep.tile([P, P], F32, name="ident")
        w1_raw = {}
        for g, (c0, c1) in enumerate(W1_GROUPS):
            for a in range(PASSES):
                tag = f"w1_raw{g}_{a}"
                w1_raw[g, a] = keep.tile([P, PACK, (c1 - c0) * P], F32, name=tag, tag=tag, align_bytes=64)

        nc.gpsimd.memset(tab_sc[:].bitcast(I32), 0)
        nc.gpsimd.memset(gain_rows[:], 0.0)
        nc.gpsimd.memset(w4_sc[:].bitcast(I32), 0)
        make_identity(nc, ident[:])

        def load_tab(a):
            nc.sync.dma_start(out=tab[a][:].bitcast(I32), in_=tab_words[a].rearrange("p n t -> p (n t)").bitcast(I32))

        def load_w1(g, passes):
            c0, c1 = W1_GROUPS[g]
            for a in passes:
                rows = w1[a * P * PACK : (a + 1) * P * PACK, c0 * P : c1 * P]
                nc.sync.dma_start(out=w1_raw[g, a][:], in_=rows.rearrange("(p t) c -> p t c", t=PACK))

        def load_page(c):
            nc.sync.dma_start(out=page[c][:], in_=page0[c * P : (c + 1) * P, :])

        def load_lap(c):
            nc.sync.dma_start(out=lap_sb[:, c, :], in_=lap[c * P : (c + 1) * P, :])

        def load_wgs(h):
            nc.sync.dma_start(out=wgs_sb[:, half_cols(h)], in_=wgs[:, half_cols(h)])

        load_tab(0)
        nc.sync.dma_start(idx1[:], offs)
        load_w1(0, [0])
        load_tab(1)
        for q in range(P // QUADRANT):
            nc.sync.dma_start(
                out=tab_sc[QUADRANT * q : QUADRANT * q + SCALE_ROWS * PASSES, :].bitcast(I32),
                in_=tab_scales[:, SCALE_ROWS * q : SCALE_ROWS * (q + 1), :].bitcast(I32),
            )
        load_tab(2)
        load_w1(0, [1, 2])
        nc.sync.dma_start(idx2[:], offs2)
        load_page(0)
        load_wgs(0)
        load_w1(1, range(PASSES))
        load_wgs(1)
        nc.sync.dma_start(idx3[:], offs3)
        load_page(1)
        load_w1(2, range(PASSES))
        load_page(2)
        nc.sync.dma_start(out=gain_rows[0:BLOCKS, :], in_=gs.rearrange("(c p) -> c p", p=P))
        nc.sync.dma_start(out=gain_rows[BLOCKS : 2 * BLOCKS, :], in_=gb.rearrange("(c p) -> c p", p=P))
        load_lap(0)
        load_lap(1)
        load_page(3)
        load_lap(2)
        load_lap(3)
        nc.sync.dma_start(out=gx_sb[:], in_=gx.rearrange("(p t) -> p t", t=PACK))
        nc.sync.dma_start(out=w4_codes[:].bitcast(I32), in_=w4_words[0].bitcast(I32))
        for q in range(P // QUADRANT):
            nc.sync.dma_start(
                out=w4_sc[QUADRANT * q : QUADRANT * q + SCALE_ROWS, :].bitcast(I32),
                in_=w4_scales[0, SCALE_ROWS * q : SCALE_ROWS * (q + 1), :].bitcast(I32),
            )
        nc.sync.dma_start(idx4[:], offs4)

        v_sc = keep.tile([P, S], U8, name="v_sc", align_bytes=64)
        v_first = keep.tile([P, S], U32, name="v_first", align_bytes=64)
        v_codes = {(0, h): v_first[:, half_cols(h)] for h in range(HALVES)}
        nc.vector.tensor_copy(v_sc[:], tab_sc[:].indirect(idx1[:]))
        nc.vector.tensor_copy(v_first[:], tab[0][:].indirect(idx1[:]))

        def gather_later_passes(h, tag):
            words = keep.tile([P, (PASSES - 1) * HALF], U32, name=f"v_later{h}", tag=tag, align_bytes=64)
            for a in range(1, PASSES):
                v_codes[a, h] = words[:, half_cols(a - 1)]
                nc.vector.tensor_copy(v_codes[a, h], tab[a][:].indirect(entries(idx1, h * HALF, HALF)))

        w1_bf, w1_codes, w1_sc = {}, {}, {}

        def round_w1(g, tag):
            c0, c1 = W1_GROUPS[g]
            width = PACK * (c1 - c0) * P
            w1_bf[g] = keep.tile([P, PASSES * width], BF16, name=f"w1_bf{g}", tag=tag, align_bytes=64)
            for a in range(PASSES):
                interleave(w1_bf[g][:, a * width : (a + 1) * width], w1_raw[g, a][:])

        def quantise_w1(g, tag):
            c0, c1 = W1_GROUPS[g]
            width = (c1 - c0) * P
            codes = keep.tile([P, PASSES * width], U32, name=f"w1_codes{g}", tag=tag, align_bytes=64)
            scales = keep.tile([P, PASSES * width], U8, name=f"w1_sc{g}", align_bytes=64)
            for a0, a1 in PASS_RUNS:
                nc.vector.quantize_mx(
                    out=codes[:, a0 * width : a1 * width].bitcast(FP8X4),
                    scales=scales[:, a0 * width : a1 * width],
                    in_=w1_bf[g][:, PACK * a0 * width : PACK * a1 * width],
                )
            for a in range(PASSES):
                for c in range(c0, c1):
                    cols = slice(a * width + (c - c0) * P, a * width + (c - c0 + 1) * P)
                    w1_codes[c, a] = codes[:, cols]
                    w1_sc[c, a] = scales[:, cols]

        def make_h(c, halves):
            banks = [psum.tile([P, HALF], F32, name="acc", tag="acc", bufs=2) for h in range(HALVES)]
            for a in range(PASSES):
                for h in range(HALVES):
                    nc.tensor.matmul_mx(
                        out=banks[h][:],
                        lhsT=w1_codes[c, a].bitcast(FP8X4),
                        lhsT_scale=w1_sc[c, a],
                        rhs=v_codes[a, h].bitcast(FP8X4),
                        rhs_scale=v_sc[SCALE_ROWS * a : P, half_cols(h)],
                        start=(a == 0),
                        stop=(a == PASSES - 1),
                    )
            for h in range(HALVES):
                nc.scalar.copy(out=halves[h], in_=banks[h][:])

        gather_later_passes(0, "v_later0")
        round_w1(0, "w1_bf0")
        quantise_w1(0, "w1_codes0")
        gather_later_passes(1, "w1_bf0")
        round_w1(1, "w1_bf1")
        h_first = [
            keep.tile([P, HALF], F32, name=f"h0_{h}", tag=tag, align_bytes=64)
            for h, tag in enumerate(("h0_0", "w1_raw1_2"))
        ]
        make_h(0, [tile[:] for tile in h_first])
        for h in range(HALVES):
            window = page[0][:].indirect(entries(idx2, h * HALF, HALF))
            nc.vector.tensor_tensor(window, h_first[h][:], wgs_sb[:, half_cols(h)], MULT)

        h_sb = {}

        def make_h_whole(c):
            h_sb[c] = keep.tile([P, S], F32, name=f"h{c}", tag=f"h{c}", align_bytes=64)
            make_h(c, [h_sb[c][:, half_cols(h)] for h in range(HALVES)])

        def scatter(c):
            nc.vector.tensor_tensor(page[c][:].indirect(idx2[:]), h_sb[c][:], wgs_sb[:], MULT)

        def pick(c, first, width, dst):
            nc.vector.tensor_copy(dst, page[c][:].indirect(entries(idx3, first, width)))

        quantise_w1(1, "h0_0")
        first_pick = keep.tile([P, HALF], F32, name="first_pick", align_bytes=64)
        pick(0, 0, HALF, first_pick[:])
        make_h_whole(1)
        scatter(1)
        round_w1(2, "h0_0")
        quantise_w1(2, "h1")
        make_h_whole(2)
        make_h_whole(3)

        gains = keep.tile([P, 2 * BLOCKS], F32, name="gains", tag="h1", align_bytes=64)
        gain_t = psum.tile([P, HALF], F32, name="z_t", bufs=2)
        nc.tensor.transpose(gain_t[:, 0:P], gain_rows[:], ident[:])
        nc.scalar.copy(out=gains[:], in_=gain_t[:, 0 : 2 * BLOCKS])

        tanh_t = keep.tile([P, NJ // P, PACK, P], F32, name="tanh_t")

        def squash(c, first, width, src):
            scaled = keep.tile([P, HALF], F32, name="scaled", bufs=4)
            nc.scalar.activation(out=scaled[:, 0:width], in_=src, func=COPY, scale=gains[:, c : c + 1])
            z_t = psum.tile([P, HALF], F32, name="z_t", bufs=2)
            terms = (lap_sb[:, c, first : first + width], scaled[:, 0:width])
            for s, term in enumerate(terms):
                for b in range(width // P):
                    nc.tensor.matmul(
                        z_t[:, b * P : (b + 1) * P],
                        lhsT=term[:, b * P : (b + 1) * P],
                        rhs=ident[:],
                        is_transpose=True,
                        start=(s == 0 and b == 0),
                        stop=(s == len(terms) - 1 and b == width // P - 1),
                    )
            per_block = P // PACK
            nc.scalar.activation(
                out=tanh_t[:, first // P : (first + width) // P, :, per_block * c : per_block * (c + 1)],
                in_=z_t[:, 0:width].rearrange("p (b q t) -> p b t q", t=PACK, q=per_block),
                func=TANH,
            )

        later_picks = keep.tile([P, HALF + NJ], F32, name="later_picks", tag="h0_0", align_bytes=64)
        pick(0, HALF, HALF, later_picks[:, 0:HALF])
        squash(0, 0, HALF, first_pick[:])
        squash(0, HALF, HALF, later_picks[:, 0:HALF])
        pick(1, 0, NJ, later_picks[:, HALF:])
        for h in range(HALVES):
            squash(1, h * HALF, HALF, later_picks[:, half_cols(h + 1)])
        scatter(2)
        picked2 = keep.tile([P, NJ], F32, name="picked2")
        pick(2, 0, NJ, picked2[:])
        for h in range(HALVES):
            squash(2, h * HALF, HALF, picked2[:, half_cols(h)])
        scatter(LAST)
        picked_last = keep.tile([P, NJ], F32, name="picked_last")
        for first, width in ((0, QUARTER), (QUARTER, QUARTER), (HALF, HALF)):
            pick(LAST, first, width, picked_last[:, first : first + width])

        side_first = keep.tile([P, BLOCKS * NJ - HALF], F32, name="side_first", tag="wgs_sb")
        for c in range(LAST):
            nc.vector.tensor_copy(side_first[:, c * NJ : (c + 1) * NJ], page[c][:].indirect(idx4[:]))
        nc.vector.tensor_copy(side_first[:, LAST * NJ :], page[LAST][:].indirect(entries(idx4, 0, HALF)))

        def round_x(first, dst):
            squash(LAST, first, QUARTER, picked_last[:, first : first + QUARTER])
            x_rows = keep.tile([P, PACK, QUARTER], BF16, name="x_rows", bufs=2)
            per_bank = HALF // QUARTER
            for t0 in range(0, PACK, per_bank):
                back = psum.tile([P, per_bank, QUARTER], F32, name="back", bufs=4)
                for e in range(per_bank):
                    for b in range(QUARTER // P):
                        nc.tensor.transpose(back[:, e, b * P : (b + 1) * P], tanh_t[:, first // P + b, t0 + e, :], ident[:])
                for e in range(per_bank):
                    t = t0 + e
                    nc.scalar.activation(out=x_rows[:, t, :], in_=back[:, e, :], func=COPY, scale=gx_sb[:, t : t + 1])
            interleave(dst, x_rows[:])

        x_codes = keep.tile([P, NJ], U32, name="x_codes", align_bytes=64)
        x_sc = keep.tile([P, NJ], U8, name="x_sc", align_bytes=64)

        def quantise_x(first, width):
            x_bf = keep.tile([P, PACK * width], BF16, name=f"x_bf{first}", tag=f"x_bf{first}", align_bytes=64)
            for u in range(width // QUARTER):
                round_x(first + u * QUARTER, x_bf[:, u * PACK * QUARTER : (u + 1) * PACK * QUARTER])
            cols = slice(first, first + width)
            nc.vector.quantize_mx(out=x_codes[:, cols].bitcast(FP8X4), scales=x_sc[:, cols], in_=x_bf[:])

        quantise_x(*X_CHUNKS[0])
        side_last = keep.tile([P, HALF], F32, name="side_last", tag="x_bf0", align_bytes=64)
        nc.vector.tensor_copy(side_last[:], page[LAST][:].indirect(entries(idx4, HALF, HALF)))
        for chunk in X_CHUNKS[1:]:
            quantise_x(*chunk)

        def side(c, first, width):
            if c == LAST and first >= HALF:
                return side_last[:, first - HALF : first - HALF + width]
            return side_first[:, c * NJ + first : c * NJ + first + width]

        weighed = {}

        def weigh(first, width, c0):
            cols = slice(first, first + width)
            count = HALF // width
            bank = psum.tile([P, HALF], F32, name="y", tag="acc", bufs=2)
            for e in range(count):
                c = c0 + e
                nc.tensor.matmul_mx(
                    out=bank[:, e * width : (e + 1) * width],
                    lhsT=w4_codes[:, 2 * c * P : 2 * (c + 1) * P].bitcast(FP4X4),
                    lhsT_scale=w4_sc[:, c * P : (c + 1) * P],
                    rhs=x_codes[:, cols].bitcast(FP8X4),
                    rhs_scale=x_sc[:, cols],
                    start=True,
                    stop=True,
                )
            product = keep.tile([P, HALF], F32, name="product", bufs=3)
            nc.vector.tensor_tensor(
                product[:].rearrange("p (e j) -> p e j", e=count),
                bank[:].rearrange("p (e j) -> p e j", e=count),
                lap_sb[:, c0 : c0 + count, cols],
                MULT,
            )
            for e in range(count):
                weighed[first, c0 + e] = product[:, e * width : (e + 1) * width]

        def finish(first, width, c0):
            for c in range(c0, c0 + HALF // width):
                res = keep.tile([P, HALF], F32, name="res", bufs=6)
                nc.vector.scalar_tensor_tensor(
                    out=res[:, 0:width],
                    in0=side(c, first, width),
                    scalar=gains[:, BLOCKS + c : BLOCKS + c + 1],
                    in1=weighed[first, c],
                    op0=MULT,
                    op1=ADD,
                )
                nc.sync.dma_start(out=out[c * P : (c + 1) * P, first : first + width], in_=res[:, 0:width])

        steps = [(first, width, c0) for first, width in X_CHUNKS for c0 in range(0, BLOCKS, HALF // width)]
        for i, step in enumerate(steps):
            weigh(*step)
            if i > 0:
                finish(*steps[i - 1])
        finish(*steps[-1])
